import numpy as np
import ml_dtypes


def mxq(x, axis, fmt="e4m3"):
    dtype, down = {"e4m3": (ml_dtypes.float8_e4m3fn, 7), "e5m2": (ml_dtypes.float8_e5m2, 14)}[fmt]
    v = np.moveaxis(np.asarray(x, np.float32).astype(ml_dtypes.bfloat16).astype(np.float64), axis, -1)
    blocks = v.reshape(v.shape[:-1] + (-1, 32))
    amax = np.abs(blocks).max(-1, keepdims=True)
    byte = np.maximum(np.where(amax > 0, np.frexp(amax)[1] - 1 + 127, 0) - down, 1)
    scale = np.exp2(byte - 127.0)
    codes = (blocks / scale).astype(np.float32).astype(dtype).astype(np.float64)
    return np.moveaxis((codes * scale).reshape(v.shape), -1, axis)


WIDE = False


def mx_kscale(k):
    if not WIDE:
        return np.ones(k)
    levels = np.array([10, -10, 5, -5, 0])
    if k % 512:
        return np.exp2(np.random.permutation(np.resize(levels, k // 32))).repeat(32)
    a = np.empty((k // 512, 16))
    for p in range(k // 512):
        a[p, :8] = np.random.permutation(np.resize(levels, 8))
        for g in range(8):
            far = levels[np.abs(levels - a[p, g]) >= 10]
            a[p, g + 8] = far[np.random.randint(len(far))]
    return np.exp2(a.ravel()).repeat(32)


BF16 = ml_dtypes.bfloat16


def bf(x):
    return np.asarray(x, np.float32).astype(BF16)


def f64(x):
    return np.asarray(x).astype(np.float64)


E2M1 = np.array([0.0, 0.5, 1.0, 1.5, 2.0, 3.0, 4.0, 6.0, -0.0, -0.5, -1.0, -1.5, -2.0, -3.0, -4.0, -6.0])


def pack_weight(w, fmt):
    k, n = w.shape
    w = f64(bf(w)).reshape(k // 32, 32, n)
    amax = np.abs(w).max(1)
    if fmt == "e4m3":
        byte = np.frexp(amax)[1] - 1 + 127 - 7
    else:
        mant, ex = np.frexp(amax / 6.0)
        byte = np.where(mant > 0.5, ex, ex - 1) + 127
    byte = np.clip(np.where(amax > 0, byte, 1), 1, 254)
    scaled = (w * np.exp2(127.0 - byte)[:, None, :]).reshape(k, n).astype(np.float32)
    by_word = np.ascontiguousarray(scaled.reshape(k // 512, 128, 4, n).transpose(0, 1, 3, 2))
    if fmt == "e4m3":
        words = by_word.astype(ml_dtypes.float8_e4m3fn).view(np.uint8)
    else:
        c = by_word.astype(ml_dtypes.float4_e2m1fn).view(np.uint8) & 0xF
        words = c[..., 0::2] | (c[..., 1::2] << 4)
    return np.ascontiguousarray(words), np.ascontiguousarray(byte.astype(np.uint8).reshape(k // 512, 16, n))


def unpack_weight(words, scales, fmt):
    g, p, n, _ = words.shape
    if fmt == "e4m3":
        vals = np.ascontiguousarray(words).view(ml_dtypes.float8_e4m3fn).astype(np.float64)
    else:
        nib = np.empty((g, p, n, 4), np.uint8)
        nib[..., 0::2] = words & 0xF
        nib[..., 1::2] = words >> 4
        vals = E2M1[nib]
    vals = vals * np.repeat(np.exp2(scales.astype(np.float64) - 127.0), 8, axis=1)[..., None]
    return vals.transpose(0, 1, 3, 2).reshape(g * 512, n)
def pack4(w):
    words, scales = pack_weight(w, "e2m1")
    return words.reshape(words.shape[0], 128, -1), scales


def unpack4(words, scales):
    return unpack_weight(words.reshape(words.shape[0], 128, -1, 2), scales, "e2m1")


H, W, C, F, R, B = 32, 64, 1024, 1024, 4, 32


def setup_inputs():
    s = mx_kscale(C)
    t = mx_kscale(F)
    x = np.random.standard_normal((C, H * W)) * s[:, None]
    wa = np.random.standard_normal((C, F)) / np.sqrt(C) / s[:, None]
    wv = np.random.standard_normal((C, F)) / np.sqrt(C) / s[:, None] * t
    wo = np.random.standard_normal((F, R * R * B)) / np.sqrt(F) / t[:, None]
    x_words, x_scales = pack4(x)
    wa_words, wa_scales = pack4(wa)
    wv_words, wv_scales = pack4(wv)
    wo_words, wo_scales = pack4(wo)
    return {"x_words": x_words, "x_scales": x_scales,
            "wa_words": wa_words, "wa_scales": wa_scales,
            "wv_words": wv_words, "wv_scales": wv_scales,
            "wo_words": wo_words, "wo_scales": wo_scales,
            "gamma": bf(1 + 0.1 * np.random.standard_normal(F)),
            "ba": bf(0.3 * np.random.standard_normal(F)),
            "bv": bf(0.3 * np.random.standard_normal(F) * t),
            "bo": bf(0.2 * np.random.standard_normal(R * R * B)),
            "alpha": bf(1 + 0.1 * np.random.standard_normal(B)),
            "base": bf(0.5 * np.random.standard_normal((H, W, B)))}


def reference(x_words, x_scales, wa_words, wa_scales, wv_words, wv_scales, wo_words, wo_scales,
              gamma, ba, bv, bo, alpha, base):
    x = unpack4(x_words, x_scales)
    a = x.T @ unpack4(wa_words, wa_scales)
    v = (x.T @ unpack4(wv_words, wv_scales)) + f64(bv)
    h = v * np.tanh(f64(gamma) * a + f64(ba))
    o = (mxq(h, 1, "e4m3") @ unpack4(wo_words, wo_scales)) + f64(bo)
    detail = np.tanh(o).reshape(H, W, R, R, B)
    y = f64(base)[:, :, None, None, :] + f64(alpha) * detail
    return y.transpose(0, 2, 1, 3, 4).reshape(H * R, W * R, B)

from contextlib import ExitStack

import concourse.mybir as mybir

F32 = mybir.dt.float32
BF16 = mybir.dt.bfloat16
I32 = mybir.dt.int32
U32 = mybir.dt.uint32
U8 = mybir.dt.uint8
FP4X4 = mybir.dt.float4_e2m1fn_x4
FP8X4 = mybir.dt.float8_e4m3fn_x4
ACT = mybir.ActivationFunctionType
ALU = mybir.AluOpType

P = 128
N_PX = 2048
N_CH = 1024
FLOPS = 2 * N_PX * 1024 * 1024 * 2 + 2 * N_PX * 1024 * 512

BLOCKS = [(0, 512), (512, 512), (1024, 512), (1536, 256), (1792, 256)]


def tile_gated_superres_head_f2_kernel(
    tc, x_words, x_scales, wa_words, wa_scales, wv_words, wv_scales, wo_words, wo_scales,
    gamma, ba, bv, bo, alpha, base, out,
):
    nc = tc.nc
    with ExitStack() as ctx:
        keep = ctx.enter_context(tc.tile_pool(name="keep", bufs=1))
        tp = ctx.enter_context(tc.tile_pool(name="tp", bufs=4))
        hp = ctx.enter_context(tc.tile_pool(name="hp", bufs=3))
        qp = ctx.enter_context(tc.tile_pool(name="qp", bufs=4))
        ep = ctx.enter_context(tc.tile_pool(name="ep", bufs=2))
        psum = ctx.enter_context(tc.psum_pool(name="psum", bufs=2))
        ctx.enter_context(tc.manual_schedule())

        w_raw = keep.tile([P, 2, 2, 2048], U8, align_bytes=64)
        s_raw = keep.tile([P, 4, 1024], U8, align_bytes=64)
        w_perm = keep.tile([P, 8, 4, 256], U8, align_bytes=64)
        s_perm = keep.tile([P, 8, 4, 128], U8, align_bytes=64)
        x_cod = keep.tile([P, 2, 4096], U8, align_bytes=64)
        x_sc = keep.tile([P, 2, 2048], U8, align_bytes=64)
        wo_raw = keep.tile([P, 2, 1024], U8, align_bytes=64)
        wos_raw = keep.tile([P, 2, 512], U8, align_bytes=64)
        wo_perm = keep.tile([P, 2, 4, 256], U8, align_bytes=64)
        wos_perm = keep.tile([P, 2, 4, 128], U8, align_bytes=64)
        vec_b = keep.tile([P, 3, 2, 8], BF16, align_bytes=64)
        vec = keep.tile([P, 3, 2, 4], F32, align_bytes=64)
        sm = keep.tile([P, 32], BF16, align_bytes=64)
        sm_t = keep.tile([P, 32], BF16, align_bytes=64)
        cols = keep.tile([P, 8], F32, align_bytes=64)
        base_l = keep.tile([P, 32, 64], BF16, align_bytes=64)
        base_t = keep.tile([P, 32, 64], BF16, align_bytes=64)
        warm = keep.tile([P, 8], F32, align_bytes=64)

        def words(ap):
            return ap.bitcast(I32)

        nc.vector.memset(s_raw[:, 0:2, :].rearrange("p a b -> p (a b)").bitcast(I32), 0)
        nc.vector.memset(x_sc[:].rearrange("p a b -> p (a b)").bitcast(I32), 0)
        nc.vector.memset(s_raw[:, 2:4, :].rearrange("p a b -> p (a b)").bitcast(I32), 0)
        nc.gpsimd.memset(warm[:], 0.0)
        nc.gpsimd.memset(sm[:], 0.0)

        def load_w(w, src, fg):
            cs = slice(fg * 1024, (fg + 1) * 1024)
            nc.sync.dma_start(out=words(w_raw[:, w, :, cs]), in_=words(src[:, :, cs].rearrange("g p n -> p g n")))

        def load_x(px, width):
            cs = slice(px * 2, (px + width) * 2)
            nc.sync.dma_start(out=words(x_cod[:, :, cs]), in_=words(x_words[:, :, cs].rearrange("g p n -> p g n")))

        def load_scales(eng, dst, src, quads=(0, 1, 2, 3)):
            for q in quads:
                eng.dma_start(out=words(dst[32 * q : 32 * q + 4]), in_=words(src[:, 4 * q : 4 * q + 4, :].rearrange("g r n -> r g n")))

        def load_vec(eng, i, v):
            eng.dma_start(out=vec_b[:, i, :, 0:4], in_=v.rearrange("(g p t) -> p g t", p=128, t=4))

        load_w(0, wa_words, 0)
        load_x(0, 512)
        load_scales(nc.scalar, s_raw[:, 0:2, :], wa_scales)
        load_scales(nc.scalar, x_sc, x_scales, (0, 1))
        load_scales(nc.gpsimd, x_sc, x_scales, (2, 3))
        load_vec(nc.sync, 0, gamma)
        load_vec(nc.sync, 1, ba)
        load_vec(nc.gpsimd, 2, bv)
        load_scales(nc.sync, s_raw[:, 2:4, :], wv_scales)
        load_w(1, wv_words, 0)
        nc.scalar.activation(out=warm[:, 1:2], in_=warm[:, 0:1], func=ACT.Tanh)
        load_w(0, wa_words, 1)
        load_w(1, wv_words, 1)
        load_x(512, 512)
        load_x(1024, 1024)
        nc.gpsimd.memset(wos_raw[:].rearrange("p a b -> p (a b)").bitcast(I32), 0)
        nc.sync.dma_start(out=words(wo_raw[:]), in_=words(wo_words.rearrange("g p n -> p g n")))
        load_scales(nc.sync, wos_raw, wo_scales)
        for i in range(4):
            nc.sync.dma_start(out=base_l[32 * i : 32 * i + 32], in_=base.rearrange("y (q b) c -> q y (b c)", b=2))
        for i in range(4):
            nc.sync.dma_start(out=sm[32 * i : 32 * i + 4, :], in_=bo[128 * i : 128 * i + 128].rearrange("(j c) -> j c", c=32))
        nc.sync.dma_start(out=sm[4:128:32, :], in_=alpha.partition_broadcast(4))

        def perm_codes(ft, w0, w1):
            fg, t = divmod(ft, 4)
            nc.vector.tensor_copy(
                out=w_perm[:, ft, 2 * w0 : 2 * w1].rearrange("p x (m b) -> p x m b", b=2),
                in_=w_raw[:, w0:w1].rearrange("p w k (c t b) -> p (w k) c t b", t=4, b=2)[:, :, fg * 128 : fg * 128 + 128, t, :],
            )

        def perm_scales(ft, w0, w1):
            fg, t = divmod(ft, 4)
            nc.vector.tensor_copy(
                out=s_perm[:, ft, 2 * w0 : 2 * w1],
                in_=s_raw[:, 2 * w0 : 2 * w1].rearrange("p x (c t) -> p x c t", t=4)[:, :, fg * 128 : fg * 128 + 128, t],
            )

        def perm(ft):
            perm_codes(ft, 0, 2)
            perm_scales(ft, 0, 2)

        perm_codes(0, 0, 1)
        perm_scales(0, 0, 1)
        nc.vector.tensor_copy(out=vec[:, 0:2], in_=vec_b[:, 0:2, :, 0:4])
        perm_codes(1, 0, 1)
        perm_scales(1, 0, 1)
        perm_codes(0, 1, 2)
        perm_scales(0, 1, 2)
        nc.vector.tensor_copy(out=vec[:, 2:3], in_=vec_b[:, 2:3, :, 0:4])
        perm_codes(1, 1, 2)
        perm_scales(1, 1, 2)

        n_units = 2 * len(BLOCKS)
        h_rows = {}
        h_inter = {}
        h_codes = {}
        h_scale = {}
        d_tiles = {}
        o_banks = {}
        y_tiles = {}
        z_tiles = {}

        gates = {}

        def product(u, t, w, tag):
            b, fg = divmod(u, 2)
            px, width = BLOCKS[b]
            bank = psum.tile([P, 512], F32, tag=tag, bufs=3, name="bank")
            for k in range(2):
                nc.tensor.matmul_mx(
                    out=bank[:, 0:width],
                    lhsT=w_perm[:, fg * 4 + t, 2 * w + k, :].bitcast(FP4X4),
                    lhsT_scale=s_perm[:, fg * 4 + t, 2 * w + k, :],
                    rhs=x_cod[:, k, 2 * px : 2 * (px + width)].bitcast(FP4X4),
                    rhs_scale=x_sc[:, k, px : px + width],
                    start=(k == 0),
                    stop=(k == 1),
                )
            return bank

        def gate_path(u, t):
            b, fg = divmod(u, 2)
            width = BLOCKS[b][1]
            a_bank = product(u, t, 0, "a")
            gate = tp.tile([P, 512], F32, tag="gate", name="gate")
            nc.scalar.activation(
                out=gate[:, 0:width], in_=a_bank[:, 0:width], func=ACT.Tanh,
                scale=vec[:, 0, fg, t : t + 1], bias=vec[:, 1, fg, t : t + 1],
            )
            gates[u, t] = gate

        def value_path(u, t):
            b, fg = divmod(u, 2)
            width = BLOCKS[b][1]
            v_bank = product(u, t, 1, "v")
            if t == 0:
                h_rows[u] = hp.tile([P, 4, 512], BF16, tag="h_rows", name="h_rows", align_bytes=64)
            nc.vector.scalar_tensor_tensor(
                out=h_rows[u][:, t, 0:width], in0=v_bank[:, 0:width], scalar=vec[:, 2, fg, t : t + 1],
                in1=gates[u, t][:, 0:width], op0=ALU.add, op1=ALU.mult,
            )

        def interleave(u, piece):
            width = BLOCKS[u // 2][1]
            n = width // 4
            if piece == 0:
                h_inter[u] = hp.tile([P, 512, 4], BF16, tag="h_inter", name="h_inter", align_bytes=64)
            dst = h_inter[u][:, piece * n : piece * n + n, :]
            src = h_rows[u][:, :, piece * n : piece * n + n].rearrange("p t n -> p n t")
            if u == n_units - 1 and piece % 2 == 0:
                nc.vector.tensor_copy(out=dst, in_=src)
            else:
                nc.scalar.copy(out=dst, in_=src)

        def quantize(u):
            width = BLOCKS[u // 2][1]
            h_codes[u] = qp.tile([P, 512], U32, tag="h_codes", name="h_codes", align_bytes=64)
            h_scale[u] = qp.tile([P, 512], U8, tag="h_scale", name="h_scale", align_bytes=64)
            nc.vector.quantize_mx(
                out=h_codes[u][:, 0:width].bitcast(FP8X4), scales=h_scale[u][:, 0:width],
                in_=h_inter[u][:, 0:width, :].rearrange("p n t -> p (n t)"),
            )

        def stage2(b, j):
            width = BLOCKS[b][1]
            n = 512 if width == 512 else 128
            o_banks[b, j] = psum.tile([P, 512], F32, tag="o", bufs=2, name="o_bank")
            for c in range(0, width, n):
                for k in range(2):
                    nc.tensor.matmul_mx(
                        out=o_banks[b, j][:, c : c + n],
                        lhsT=wo_perm[:, k, j, :].bitcast(FP4X4),
                        lhsT_scale=wos_perm[:, k, j, :],
                        rhs=h_codes[2 * b + k][:, c : c + n].bitcast(FP8X4),
                        rhs_scale=h_scale[2 * b + k][:, c : c + n],
                        start=(k == 0),
                        stop=(k == 1),
                    )

        def detail(b, j):
            width = BLOCKS[b][1]
            d_tiles[b, j] = ep.tile([P, 512], F32, tag="detail", bufs=3, name="d_tile")
            nc.scalar.activation(
                out=d_tiles[b, j][:, 0:width].rearrange("p (y b q) -> p y b q", b=2, q=32),
                in_=o_banks[b, j][:, 0:width].rearrange("p (y q b) -> p y b q", b=2, q=32),
                func=ACT.Tanh, bias=cols[:, j : j + 1],
            )

        def blend(b, j):
            px, width = BLOCKS[b]
            nb = width // 32
            if j == 0:
                y_tiles[b] = ep.tile([P, 16, 4, 32], F32, tag="y", name="y_tile", align_bytes=64)
            nc.vector.scalar_tensor_tensor(
                out=y_tiles[b][:, 0:nb, j, :],
                in0=d_tiles[b, j][:, 0:width].rearrange("p (b q) -> p b q", q=32),
                scalar=cols[:, 4:5],
                in1=base_t[:].rearrange("p y (b q) -> p (y b) q", q=32)[:, px // 32 : px // 32 + nb, :],
                op0=ALU.mult, op1=ALU.add,
            )

        out_rows = out.rearrange("r w c -> (r w c)").rearrange("(y p n) -> p y n", p=128, n=256)

        def turn_and_store(b, half):
            px, width = BLOCKS[b]
            if half == 0:
                z_tiles[b] = ep.tile([P, 8, 256], F32, tag="z", name="z_tile", align_bytes=64)
            nb = width // 64
            ny = width // 128
            bs = slice(half * nb, half * nb + nb)
            ys = slice(half * ny, half * ny + ny)
            nc.vector.transpose(
                out=z_tiles[b][:, ys, :].rearrange("p y n -> p (y n)"),
                in_=y_tiles[b][:, bs].rearrange("p b j q -> p (b j q)"),
            )
            y0 = px // 64 + half * ny
            nc.sync.dma_start(out=out_rows[:, y0 : y0 + ny, :], in_=z_tiles[b][:, ys, :])

        def prepare_epilogue():
            for k in range(2):
                nc.gpsimd.tensor_copy(
                    out=wo_perm[:, k].bitcast(I32).rearrange("p j (i c) -> p j i c", i=4),
                    in_=wo_raw[:, k].bitcast(I32).rearrange("p (i j c) -> p j i c", i=4, j=4),
                )
                nc.gpsimd.tensor_copy(
                    out=wos_perm[:, k].bitcast(I32).rearrange("p j (i c) -> p j i c", i=4),
                    in_=wos_raw[:, k].bitcast(I32).rearrange("p (i j c) -> p j i c", i=4, j=4),
                )
            nc.vector.transpose(out=sm_t[:], in_=sm[:])
            nc.vector.tensor_copy(out=cols[:], in_=sm_t[:, 0:8])

        def turn_base(q):
            nc.vector.transpose(
                out=base_t[:, 8 * q : 8 * q + 8].rearrange("p y n -> p (y n)"),
                in_=base_l[:, 8 * q : 8 * q + 8].rearrange("p y n -> p (y n)"),
            )

        todo = {}

        def at(u, t, fn, *args):
            todo.setdefault(4 * u + t, []).append((fn, args))

        for ft in range(2, 8):
            at(0, ft - 2, perm, ft)
        at(1, 3, prepare_epilogue)
        for q in range(4):
            at(2, q, turn_base, q)
        for u in range(n_units):
            for piece in range(4):
                at(u + 1, piece, interleave, u, piece)
            at(u + 2, 0, quantize, u)
        for b in range(len(BLOCKS)):
            for j in range(4):
                at(2 * b + 3, 1 + j, stage2, b, j)
                at(2 * b + 3, 2 + j, detail, b, j)
                at(2 * b + 3, 3 + j, blend, b, j)
            at(2 * b + 4, 3, turn_and_store, b, 0)
            at(2 * b + 4, 4, turn_and_store, b, 1)

        for s in range(max(todo) + 1):
            if s == 0:
                gate_path(0, 0)
            if s + 1 < 4 * n_units:
                gate_path((s + 1) // 4, (s + 1) % 4)
            if s < 4 * n_units:
                value_path(s // 4, s % 4)
            for fn, args in todo.get(s, []):
                fn(*args)
